import numpy as np
import ml_dtypes


def mxq(x, axis, fmt="e4m3"):
    dtype, down = {"e4m3": (ml_dtypes.float8_e4m3fn, 7), "e5m2": (ml_dtypes.float8_e5m2, 14)}[fmt]
    v = np.moveaxis(np.asarray(x, np.float32).astype(ml_dtypes.bfloat16).astype(np.float64), axis, -1)
    blocks = v.reshape(v.shape[:-1] + (-1, 32))
    amax = np.abs(blocks).max(-1, keepdims=True)
    byte = np.maximum(np.where(amax > 0, np.frexp(amax)[1] - 1 + 127, 0) - down, 1)
    scale = np.exp2(byte - 127.0)
    codes = (blocks / scale).astype(np.float32).astype(dtype).astype(np.float64)
    return np.moveaxis((codes * scale).reshape(v.shape), -1, axis)


WIDE = False


def mx_kscale(k):
    if not WIDE:
        return np.ones(k)
    levels = np.array([10, -10, 5, -5, 0])
    if k % 512:
        return np.exp2(np.random.permutation(np.resize(levels, k // 32))).repeat(32)
    a = np.empty((k // 512, 16))
    for p in range(k // 512):
        a[p, :8] = np.random.permutation(np.resize(levels, 8))
        for g in range(8):
            far = levels[np.abs(levels - a[p, g]) >= 10]
            a[p, g + 8] = far[np.random.randint(len(far))]
    return np.exp2(a.ravel()).repeat(32)


def f64(x):
    return np.asarray(x).astype(np.float64)


def striped(idx):
    return np.tile(idx.reshape(-1, 16).T, (8, 1)).astype(np.uint16)


def unstriped(offs):
    return offs[:16].T.reshape(-1).astype(np.int64)


E2M1 = np.array([0.0, 0.5, 1.0, 1.5, 2.0, 3.0, 4.0, 6.0, -0.0, -0.5, -1.0, -1.5, -2.0, -3.0, -4.0, -6.0])


def pack_weight(w, fmt):
    k, n = w.shape
    w = f64(np.asarray(w, np.float32).astype(ml_dtypes.bfloat16)).reshape(k // 32, 32, n)
    amax = np.abs(w).max(1)
    if fmt == "e4m3":
        byte = np.frexp(amax)[1] - 1 + 127 - 7
    else:
        mant, ex = np.frexp(amax / 6.0)
        byte = np.where(mant > 0.5, ex, ex - 1) + 127
    byte = np.clip(np.where(amax > 0, byte, 1), 1, 254)
    scaled = (w * np.exp2(127.0 - byte)[:, None, :]).reshape(k, n).astype(np.float32)
    by_word = np.ascontiguousarray(scaled.reshape(k // 512, 128, 4, n).transpose(0, 1, 3, 2))
    if fmt == "e4m3":
        words = by_word.astype(ml_dtypes.float8_e4m3fn).view(np.uint8)
    else:
        c = by_word.astype(ml_dtypes.float4_e2m1fn).view(np.uint8) & 0xF
        words = (c[..., 0::2] | (c[..., 1::2] << 4)).reshape(k // 512, 128, 2 * n)
    return np.ascontiguousarray(words), np.ascontiguousarray(byte.astype(np.uint8).reshape(k // 512, 16, n))


def unpack_weight(words, scales, fmt):
    g, _, n = scales.shape
    words = np.ascontiguousarray(words).reshape(g, 128, n, -1)
    if fmt == "e4m3":
        vals = words.view(ml_dtypes.float8_e4m3fn).astype(np.float64)
    else:
        nib = np.empty((g, 128, n, 4), np.uint8)
        nib[..., 0::2] = words & 0xF
        nib[..., 1::2] = words >> 4
        vals = E2M1[nib]
    vals = vals * np.repeat(np.exp2(scales.astype(np.float64) - 127.0), 8, axis=1)[..., None]
    return vals.transpose(0, 1, 3, 2).reshape(g * 512, n)


def gelu(v):
    return 0.5 * v * (1.0 + np.tanh(np.sqrt(2.0 / np.pi) * (v + 0.044715 * v**3)))


def bf(x):
    return np.asarray(x, np.float32).astype(ml_dtypes.bfloat16)


def planes(Y):
    n, m = Y.shape
    b = f64(bf(Y)).reshape(n // 32, 32, m)
    amax = np.abs(b).max(1)
    byte = np.clip(np.where(amax > 0, np.frexp(amax)[1] - 1 + 127 - 7, 1), 1, 254)
    codes = (b * np.exp2(127.0 - byte)[:, None, :]).reshape(n, m).astype(np.float32).astype(ml_dtypes.float8_e4m3fn).view(np.uint8)
    words = codes.reshape(n // 512, 128, 4, m).transpose(0, 1, 3, 2)
    return np.ascontiguousarray(words), np.ascontiguousarray(byte.astype(np.uint8).reshape(n // 512, 16, m))


T, S, P, P2, K, H, N = 4096, 2048, 1024, 512, 1024, 1024, 512

def setup_inputs():
    n = np.random.standard_normal
    s = mx_kscale(K)[:, None]
    u = mx_kscale(H)[:, None]
    tab_words, tab_scales = pack_weight(n((K, T)) * s, "e4m3")
    w1 = (1.3 * n((K, H)) / np.sqrt(K) / s).astype(np.float32)
    b1 = (0.6 * n(H)).astype(np.float32)
    gain = (np.exp(0.3 * n(H)) * u[:, 0]).astype(np.float32)
    w4 = n((H, N)) / np.sqrt(H) * np.exp(0.8 * n(N)) / u
    w4_words, w4_scales = pack_weight(w4, "e2m1")
    offs = striped(np.random.permutation(T)[:S])
    pos1 = striped(np.random.permutation(S)[:P])
    pos2 = striped(np.random.permutation(S)[:P])
    pos3 = striped(np.random.permutation(P)[:P2])
    pos4 = striped(np.random.permutation(S)[:P2])
    return {"tab_words": tab_words, "tab_scales": tab_scales, "offs": offs,
            "pos1": pos1, "pos2": pos2, "pos3": pos3, "pos4": pos4,
            "w1": w1, "b1": b1, "gain": gain,
            "w4_words": w4_words, "w4_scales": w4_scales}

def reference(tab_words, tab_scales, offs, pos1, pos2, pos3, pos4, w1, b1, gain, w4_words, w4_scales):
    v = unpack_weight(tab_words, tab_scales, "e4m3")[:, unstriped(offs)]
    w4 = unpack_weight(w4_words, w4_scales, "e2m1")
    pre = mxq(f64(w1), 0, "e4m3").T @ v
    h = np.tanh(pre + f64(b1)[:, None]) * f64(gain)[:, None]
    a1 = np.abs(h[:, unstriped(pos1)] - h[:, unstriped(pos2)])
    a2 = a1[:, unstriped(pos3)] + h[:, unstriped(pos4)]
    y = w4.T @ mxq(a2, 0, "e4m3")
    words, scales = planes(y)
    return y, words, scales

@@ -1,0 +1,333 @@
+from contextlib import ExitStack
+
+import concourse.mybir as mybir
+
+T, S, PAIRS, KEPT, K, H, N = 4096, 2048, 1024, 512, 1024, 1024, 512
+FLOPS = 2 * K * H * S + 2 * H * N * KEPT
+
+F32 = mybir.dt.float32
+BF16 = mybir.dt.bfloat16
+I32 = mybir.dt.int32
+U32 = mybir.dt.uint32
+U16 = mybir.dt.uint16
+U8 = mybir.dt.uint8
+E4M3 = mybir.dt.float8_e4m3fn_x4
+E2M1 = mybir.dt.float4_e2m1fn_x4
+ACT = mybir.ActivationFunctionType
+ALU = mybir.AluOpType
+
+P = 128
+PACK = 4
+PASS = P * PACK
+BANK = 512
+LIST = 16
+TILES = H // P
+HALF = 256
+CHUNKS = ((0, 256), (256, 384), (384, 512))
+
+
+def tile_list_baptism_linking_features_kernel(
+    tc, tab_words, tab_scales, offs, pos1, pos2, pos3, pos4, w1, b1, gain, w4_words, w4_scales, out_0, out_1, out_2
+):
+    nc = tc.nc
+    with ExitStack() as ctx:
+        pool = ctx.enter_context(tc.tile_pool(name="sbuf", bufs=1))
+        psum = ctx.enter_context(tc.psum_pool(name="psum", bufs=8))
+
+        def sb(name, shape, dtype, tag=None, bufs=1):
+            return pool.tile(shape, dtype, name=name, tag=tag or name, bufs=bufs, align_bytes=64)
+
+        def entries(offsets, first, last):
+            return offsets[:, first // LIST : last // LIST]
+
+        idx = sb("idx", [P, S // LIST], U16)
+        nc.sync.dma_start(idx[:], offs)
+        scale_rows = sb("scale_rows", [P, T], U8)
+        nc.sync.dma_start(scale_rows[0:32, :].bitcast(I32), tab_scales.rearrange("a q t -> (a q) t").bitcast(I32))
+        nc.vector.memset(scale_rows[32:64, :].bitcast(I32), 0)
+        nc.vector.memset(scale_rows[64:128, :].bitcast(I32), 0)
+
+        gain_t = sb("gain_t", [P, TILES], F32)
+        bias_t = sb("bias_t", [P, TILES], F32)
+        nc.gpsimd.dma_start(gain_t[:].rearrange("p (b t) -> p b t", t=PACK), gain.rearrange("(b p t) -> p b t", p=P, t=PACK))
+        nc.gpsimd.dma_start(bias_t[:].rearrange("p (b t) -> p b t", t=PACK), b1.rearrange("(b p t) -> p b t", p=P, t=PACK))
+
+        table = [sb(f"table{a}", [P, T], I32) for a in range(2)]
+        w1_raw = {}
+
+        def load_table(a):
+            nc.sync.dma_start(table[a][:], tab_words[a].rearrange("p t i -> p (t i)").bitcast(I32))
+
+        def load_w1(b, a):
+            w1_raw[b, a] = sb(f"w1_raw{b}{a}", [P, PACK, PASS], F32, tag="wide", bufs=6)
+            rows = w1[a * PASS : (a + 1) * PASS, b * PASS : (b + 1) * PASS]
+            nc.sync.dma_start(w1_raw[b, a][:], rows.rearrange("(p j) c -> p j c", j=PACK))
+
+        load_table(0)
+        load_w1(0, 0)
+        load_table(1)
+        load_w1(0, 1)
+        p1 = sb("p1", [P, PAIRS // LIST], U16)
+        p2 = sb("p2", [P, PAIRS // LIST], U16)
+        p3 = sb("p3", [P, KEPT // LIST], U16)
+        p4 = sb("p4", [P, KEPT // LIST], U16)
+        nc.sync.dma_start(p1[:], pos1)
+        nc.sync.dma_start(p2[:], pos2)
+        nc.sync.dma_start(p4[:], pos4)
+        nc.sync.dma_start(p3[:], pos3)
+        w4_raw = sb("w4_raw", [P, 2, 2 * N], U8)
+        nc.sync.dma_start(w4_raw[:].bitcast(I32), w4_words.rearrange("a p c -> p a c").bitcast(I32))
+        load_w1(1, 0)
+        load_w1(1, 1)
+
+        v_scales = [sb(f"v_scales{a}", [P, S], U8) for a in range(2)]
+        for a in range(2):
+            nc.gpsimd.memset(v_scales[a][:].bitcast(I32), 0)
+        w4_raw_scales = sb("w4_raw_scales", [P, 2, N], U8)
+        nc.gpsimd.memset(w4_raw_scales[:].bitcast(I32), 0)
+        for q in range(4):
+            nc.sync.dma_start(
+                w4_raw_scales[32 * q : 32 * q + 4, :, :].bitcast(I32),
+                w4_scales[:, 4 * q : 4 * q + 4, :].rearrange("a r c -> r a c").bitcast(I32),
+            )
+
+        gain_wide = sb("gain_wide", [P, TILES, HALF], F32)
+        nc.scalar.copy(gain_wide[:], gain_t[:].unsqueeze(2).to_broadcast([P, TILES, HALF]))
+
+        picked_rows = sb("picked_rows", [P, S], U8)
+        nc.vector.tensor_copy(picked_rows[:], scale_rows[:].indirect(idx[:]))
+        for a in range(2):
+            for q in range(4):
+                nc.gpsimd.dma_start(
+                    v_scales[a][32 * q : 32 * q + 4, :].bitcast(I32),
+                    picked_rows[16 * a + 4 * q : 16 * a + 4 * q + 4, :].bitcast(I32),
+                )
+        v_words0 = sb("v_words0", [P, S], U32)
+        nc.vector.tensor_copy(v_words0[:], table[0][:].bitcast(U32).indirect(idx[:]))
+
+        w1_codes = {(b, a): sb(f"w1_codes{b}{a}", [P, PASS], U32) for b in range(2) for a in range(2)}
+        w1_scales = {(b, a): sb(f"w1_scales{b}{a}", [P, PASS], U8) for b in range(2) for a in range(2)}
+
+        def round_w1(copy, rounded, b, a, t0, t1, m0, m1):
+            copy(
+                rounded[:].rearrange("p (t m j) -> p m j t", m=P, j=PACK)[:, m0:m1],
+                w1_raw[b, a][:].rearrange("p j (m t) -> p m j t", t=PACK)[:, m0:m1, :, t0:t1],
+            )
+
+        def quantise_w1(rounded, b, a, t0, t1):
+            cols = slice(t0 * P, t1 * P)
+            nc.vector.quantize_mx(out=w1_codes[b, a][:, cols].bitcast(E4M3), scales=w1_scales[b, a][:, cols], in_=rounded[:])
+
+        rounded00 = sb("rounded00", [P, PACK * PASS], BF16, tag="rounded", bufs=2)
+        round_w1(nc.scalar.copy, rounded00, 0, 0, 0, PACK, 0, P)
+        quantise_w1(rounded00, 0, 0, 0, PACK)
+
+        v_words1 = []
+
+        def gather_words1(c, tag):
+            v_words1.append(sb(f"v_words1_{c}", [P, BANK], U32, tag=tag))
+            nc.vector.tensor_copy(v_words1[c][:], table[1][:].bitcast(U32).indirect(entries(idx, c * BANK, (c + 1) * BANK)))
+
+        for c in range(3):
+            gather_words1(c, None)
+        rounded_first = sb("rounded_first", [P, PASS], BF16, tag="first")
+        round_w1(nc.scalar.copy, rounded_first, 0, 1, 0, 1, 0, P)
+        quantise_w1(rounded_first, 0, 1, 0, 1)
+        gather_words1(3, "first")
+        rounded_rest = sb("rounded_rest", [P, 3 * PASS], BF16, tag="table1")
+        round_w1(nc.vector.tensor_copy, rounded_rest, 0, 1, 1, PACK, 0, P)
+        quantise_w1(rounded_rest, 0, 1, 1, PACK)
+
+        th = {}
+
+        def first_stage(i):
+            b, t = divmod(i, PACK)
+            cols = slice(t * P, (t + 1) * P)
+            th[i] = sb(f"th{i}", [P, S], F32, tag="wide", bufs=6)
+            for c in range(S // BANK):
+                span = slice(c * BANK, (c + 1) * BANK)
+                acc = psum.tile([P, BANK], F32, name=f"pre{i}_{c}", tag="bank")
+                for a, words in enumerate((v_words0[:, span], v_words1[c][:])):
+                    nc.tensor.matmul_mx(
+                        out=acc[:],
+                        lhsT=w1_codes[b, a][:, cols].bitcast(E4M3),
+                        lhsT_scale=w1_scales[b, a][:, cols],
+                        rhs=words.bitcast(E4M3),
+                        rhs_scale=v_scales[a][:, span],
+                        start=(a == 0),
+                        stop=(a == 1),
+                    )
+                nc.scalar.activation(th[i][:, span], acc[:], ACT.Tanh, bias=bias_t[:, i : i + 1])
+
+        diff, a1, burial = {}, {}, {}
+
+        def gather_burial(out, i, j0, j1):
+            nc.vector.tensor_tensor(out, th[i][:].indirect(entries(p4, j0, j1)), gain_wide[:, i, 0 : j1 - j0], ALU.mult)
+
+        def gather_pairs(i):
+            one = sb(f"one{i}", [P, PAIRS], F32, tag=f"one{i % 2}")
+            diff[i] = sb(f"diff{i}", [P, PAIRS], F32, tag="diff", bufs=2)
+            if i < PACK:
+                burial[i] = sb(f"burial{i}", [P, KEPT], F32, tag="burial", bufs=2)
+                nc.vector.tensor_copy(one[:], th[i][:].indirect(p1[:]))
+                for j0 in range(0, KEPT, HALF):
+                    gather_burial(burial[i][:, j0 : j0 + HALF], i, j0, j0 + HALF)
+                nc.vector.tensor_tensor(diff[i][:], th[i][:].indirect(p2[:]), one[:], ALU.subtract)
+            else:
+                halves = [(m0, m0 + PAIRS // 2) for m0 in range(0, PAIRS, PAIRS // 2)]
+                for m0, m1 in halves:
+                    nc.vector.tensor_copy(one[:, m0:m1], th[i][:].indirect(entries(p1, m0, m1)))
+                for m0, m1 in halves:
+                    nc.vector.tensor_tensor(diff[i][:, m0:m1], th[i][:].indirect(entries(p2, m0, m1)), one[:, m0:m1], ALU.subtract)
+
+        def absolute(i):
+            a1[i] = sb(f"a1_{i}", [P, PAIRS], F32, tag="a1", bufs=5)
+            nc.scalar.activation(a1[i][:], diff[i][:], ACT.Abs, scale=gain_t[:, i : i + 1])
+
+        def interleave(copy, rounded, planes):
+            copy(rounded.rearrange("p (c i t) -> p c t i", i=4, t=PACK), planes.rearrange("p t (c i) -> p c t i", i=4))
+
+        a2_first = sb("a2_first", [P, PACK, KEPT], F32)
+
+        def join_first(i):
+            nc.vector.tensor_tensor(a2_first[:, i, :], a1[i][:].indirect(p3[:]), burial[i][:], ALU.add)
+
+        def prepare_w1_second():
+            for a in range(2):
+                rounded = sb(f"rounded1{a}", [P, PACK * PASS], BF16, tag="rounded", bufs=2)
+                for m0 in range(0, P, P // 2):
+                    round_w1(nc.scalar.copy, rounded, 1, a, 0, PACK, m0, m0 + P // 2)
+                quantise_w1(rounded, 1, a, 0, PACK)
+
+        w4_codes = sb("w4_codes", [P, 2, 2 * N], U8)
+        w4_planes = sb("w4_planes", [P, 2, N], U8)
+
+        def deal_w4():
+            nc.vector.tensor_copy(
+                w4_planes[:].rearrange("p a (t m) -> p a t m", t=PACK),
+                w4_raw_scales[:].rearrange("p a (m t) -> p a t m", t=PACK),
+            )
+            nc.scalar.copy(
+                w4_codes[:].bitcast(U16).rearrange("p a (t m) -> p a t m", t=PACK),
+                w4_raw[:].bitcast(U16).rearrange("p a (m t) -> p a t m", t=PACK),
+            )
+
+        y_banks = {}
+
+        def second_stage(b, codes, scales, j0, j1):
+            for jb in range(j0, j1, P):
+                if b == 0:
+                    y_banks[jb] = psum.tile([P, BANK], F32, name=f"y{jb}", tag="bank")
+                cols = slice(jb - j0, jb - j0 + P)
+                for t in range(PACK):
+                    nc.tensor.matmul_mx(
+                        out=y_banks[jb][:, t * P : (t + 1) * P],
+                        lhsT=w4_codes[:, b, 2 * t * P : 2 * (t + 1) * P].bitcast(E2M1),
+                        lhsT_scale=w4_planes[:, b, t * P : (t + 1) * P],
+                        rhs=codes[:, cols].bitcast(E4M3),
+                        rhs_scale=scales[:, cols],
+                        start=(b == 0 and t == 0),
+                        stop=(b == 1 and t == PACK - 1),
+                    )
+
+        def quantise_a2(name, rounded, width):
+            codes = sb(f"{name}_codes", [P, width], U32)
+            scales = sb(f"{name}_scales", [P, width], U8)
+            nc.vector.quantize_mx(out=codes[:].bitcast(E4M3), scales=scales[:], in_=rounded[:])
+            return codes, scales
+
+        def first_pass_of_second_stage():
+            rounded = sb("a2_first_rounded", [P, PACK * KEPT], BF16, tag="rounded", bufs=2)
+            for j0 in range(0, KEPT, HALF):
+                interleave(nc.scalar.copy, rounded[:, PACK * j0 : PACK * (j0 + HALF)], a2_first[:, :, j0 : j0 + HALF])
+            codes, scales = quantise_a2("a2_first", rounded, KEPT)
+            second_stage(0, codes, scales, 0, KEPT)
+
+        first_stage(0)
+        first_stage(1)
+        for i in range(TILES):
+            gather_pairs(i)
+            if 1 <= i <= PACK:
+                join_first(i - 1)
+            if i + 2 < TILES:
+                first_stage(i + 2)
+            absolute(i)
+            if i == 0:
+                prepare_w1_second()
+            if i == 1:
+                deal_w4()
+            if i == 5:
+                first_pass_of_second_stage()
+
+        y_codes = sb("y_codes", [P, KEPT], U32)
+        y_scales = sb("y_scales", [P, KEPT], U8)
+        out_rows = out_0.rearrange("(p t) j -> p t j", t=PACK)
+        out_words = out_1[0].rearrange("p m t -> p (m t)").bitcast(I32)
+        held, joined, rounded_a2, rounded_y = {}, {}, {}, {}
+
+        def burial_chunk(c):
+            j0, j1 = CHUNKS[c]
+            held[c] = sb(f"held{c}", [P, PACK, j1 - j0], F32, tag="one1")
+            for t in range(PACK):
+                gather_burial(held[c][:, t, :], PACK + t, j0, j1)
+
+        def join_chunk(c):
+            j0, j1 = CHUNKS[c]
+            joined[c] = sb(f"joined{c}", [P, PACK, j1 - j0], F32, tag=f"chain{c}")
+            for t in range(PACK):
+                nc.vector.tensor_tensor(joined[c][:, t, :], a1[PACK + t][:].indirect(entries(p3, j0, j1)), held[c][:, t, :], ALU.add)
+
+        def round_chunk(c, copy):
+            j0, j1 = CHUNKS[c]
+            rounded_a2[c] = sb(f"rounded_a2_{c}", [P, PACK * (j1 - j0)], BF16, tag=f"chain{c + 1}")
+            interleave(copy, rounded_a2[c][:], joined[c][:])
+
+        def multiply_chunk(c):
+            j0, j1 = CHUNKS[c]
+            codes, scales = quantise_a2(f"a2_{c}", rounded_a2[c], j1 - j0)
+            second_stage(1, codes, scales, j0, j1)
+
+        def round_y(c, copy):
+            j0, j1 = CHUNKS[c]
+            rounded_y[c] = sb(f"rounded_y{c}", [P, PACK * (j1 - j0)], BF16)
+            for jb in range(j0, j1, P):
+                copy(
+                    rounded_y[c][:, PACK * (jb - j0) : PACK * (jb - j0 + P)].rearrange("p (j t) -> p j t", t=PACK),
+                    y_banks[jb][:].rearrange("p (t j) -> p j t", t=PACK),
+                )
+
+        def quantise_y(c):
+            j0, j1 = CHUNKS[c]
+            nc.vector.quantize_mx(out=y_codes[:, j0:j1].bitcast(E4M3), scales=y_scales[:, j0:j1], in_=rounded_y[c][:])
+            nc.sync.dma_start(out_words[:, j0:j1], y_codes[:, j0:j1].bitcast(I32))
+
+        def store_y(c, queue):
+            j0, j1 = CHUNKS[c]
+            y = sb(f"y_out{c}", [P, PACK, j1 - j0], F32)
+            for jb in range(j0, j1, P):
+                nc.scalar.copy(y[:, :, jb - j0 : jb - j0 + P], y_banks[jb][:].rearrange("p (t j) -> p t j", t=PACK))
+            queue.dma_start(out_rows[:, :, j0:j1], y[:])
+
+        burial_chunk(0)
+        join_chunk(0)
+        round_chunk(0, nc.scalar.copy)
+        burial_chunk(1)
+        multiply_chunk(0)
+        join_chunk(1)
+        round_chunk(1, nc.scalar.copy)
+        round_y(0, nc.scalar.copy)
+        burial_chunk(2)
+        quantise_y(0)
+        multiply_chunk(1)
+        join_chunk(2)
+        round_y(1, nc.scalar.copy)
+        store_y(0, nc.sync)
+        round_chunk(2, nc.vector.tensor_copy)
+        quantise_y(1)
+        multiply_chunk(2)
+        store_y(1, nc.sync)
+        round_y(2, nc.vector.tensor_copy)
+        store_y(2, nc.scalar)
+        quantise_y(2)
+        for q in range(4):
+            nc.sync.dma_start(out_2[0, 4 * q : 4 * q + 4, :].bitcast(I32), y_scales[32 * q : 32 * q + 4, :].bitcast(I32))

@@ -42,10 +42,18 @@ def tile_list_baptism_linking_features_kernel(
 
         idx = sb("idx", [P, S // LIST], U16)
         nc.sync.dma_start(idx[:], offs)
-        scale_rows = sb("scale_rows", [P, T], U8)
+        scale_rows = sb("scale_rows", [P, T], U8, tag="scale_rows")
         nc.sync.dma_start(scale_rows[0:32, :].bitcast(I32), tab_scales.rearrange("a q t -> (a q) t").bitcast(I32))
         nc.vector.memset(scale_rows[32:64, :].bitcast(I32), 0)
         nc.vector.memset(scale_rows[64:128, :].bitcast(I32), 0)
+        p1 = sb("p1", [P, PAIRS // LIST], U16)
+        p2 = sb("p2", [P, PAIRS // LIST], U16)
+        p3 = sb("p3", [P, KEPT // LIST], U16)
+        p4 = sb("p4", [P, KEPT // LIST], U16)
+        nc.sync.dma_start(p1[:], pos1)
+        nc.sync.dma_start(p2[:], pos2)
+        nc.sync.dma_start(p4[:], pos4)
+        nc.sync.dma_start(p3[:], pos3)
 
         gain_t = sb("gain_t", [P, TILES], F32)
         bias_t = sb("bias_t", [P, TILES], F32)
@@ -58,52 +66,42 @@ def tile_list_baptism_linking_features_kernel(
         def load_table(a):
             nc.sync.dma_start(table[a][:], tab_words[a].rearrange("p t i -> p (t i)").bitcast(I32))
 
-        def load_w1(b, a):
-            w1_raw[b, a] = sb(f"w1_raw{b}{a}", [P, PACK, PASS], F32, tag="wide", bufs=6)
+        def load_w1(b, a, raw):
+            w1_raw[b, a] = raw
             rows = w1[a * PASS : (a + 1) * PASS, b * PASS : (b + 1) * PASS]
-            nc.sync.dma_start(w1_raw[b, a][:], rows.rearrange("(p j) c -> p j c", j=PACK))
+            nc.sync.dma_start(raw, rows.rearrange("(p j) c -> p j c", j=PACK))
 
         load_table(0)
-        load_w1(0, 0)
+        load_w1(0, 0, sb("w1_raw00", [P, PACK, PASS], F32, tag="wide", bufs=5)[:])
         load_table(1)
-        load_w1(0, 1)
-        p1 = sb("p1", [P, PAIRS // LIST], U16)
-        p2 = sb("p2", [P, PAIRS // LIST], U16)
-        p3 = sb("p3", [P, KEPT // LIST], U16)
-        p4 = sb("p4", [P, KEPT // LIST], U16)
-        nc.sync.dma_start(p1[:], pos1)
-        nc.sync.dma_start(p2[:], pos2)
-        nc.sync.dma_start(p4[:], pos4)
-        nc.sync.dma_start(p3[:], pos3)
-        w4_raw = sb("w4_raw", [P, 2, 2 * N], U8)
-        nc.sync.dma_start(w4_raw[:].bitcast(I32), w4_words.rearrange("a p c -> p a c").bitcast(I32))
-        load_w1(1, 0)
-        load_w1(1, 1)
 
         v_scales = [sb(f"v_scales{a}", [P, S], U8) for a in range(2)]
         for a in range(2):
             nc.gpsimd.memset(v_scales[a][:].bitcast(I32), 0)
-        w4_raw_scales = sb("w4_raw_scales", [P, 2, N], U8)
-        nc.gpsimd.memset(w4_raw_scales[:].bitcast(I32), 0)
-        for q in range(4):
-            nc.sync.dma_start(
-                w4_raw_scales[32 * q : 32 * q + 4, :, :].bitcast(I32),
-                w4_scales[:, 4 * q : 4 * q + 4, :].rearrange("a r c -> r a c").bitcast(I32),
-            )
 
         gain_wide = sb("gain_wide", [P, TILES, HALF], F32)
         nc.scalar.copy(gain_wide[:], gain_t[:].unsqueeze(2).to_broadcast([P, TILES, HALF]))
 
         picked_rows = sb("picked_rows", [P, S], U8)
         nc.vector.tensor_copy(picked_rows[:], scale_rows[:].indirect(idx[:]))
-        for a in range(2):
+
+        def move_scale_rows(a, queue):
             for q in range(4):
-                nc.gpsimd.dma_start(
+                queue.dma_start(
                     v_scales[a][32 * q : 32 * q + 4, :].bitcast(I32),
                     picked_rows[16 * a + 4 * q : 16 * a + 4 * q + 4, :].bitcast(I32),
                 )
+
+        move_scale_rows(0, nc.scalar)
+        load_w1(0, 1, sb("w1_raw01", [P, PACK, PASS], F32, tag="scale_rows")[:])
+        move_scale_rows(1, nc.sync)
         v_words0 = sb("v_words0", [P, S], U32)
         nc.vector.tensor_copy(v_words0[:], table[0][:].bitcast(U32).indirect(idx[:]))
+        w1_second = sb("w1_second", [P, 2, PACK, PASS], F32, tag="table0")
+        for a in range(2):
+            load_w1(1, a, w1_second[:, a])
+        w4_raw = sb("w4_raw", [P, 2, 2 * N], U8, tag="picked_rows")
+        nc.sync.dma_start(w4_raw[:].bitcast(I32), w4_words.rearrange("a p c -> p a c").bitcast(I32))
 
         w1_codes = {(b, a): sb(f"w1_codes{b}{a}", [P, PASS], U32) for b in range(2) for a in range(2)}
         w1_scales = {(b, a): sb(f"w1_scales{b}{a}", [P, PASS], U8) for b in range(2) for a in range(2)}
@@ -111,16 +109,23 @@ def tile_list_baptism_linking_features_kernel(
         def round_w1(copy, rounded, b, a, t0, t1, m0, m1):
             copy(
                 rounded[:].rearrange("p (t m j) -> p m j t", m=P, j=PACK)[:, m0:m1],
-                w1_raw[b, a][:].rearrange("p j (m t) -> p m j t", t=PACK)[:, m0:m1, :, t0:t1],
+                w1_raw[b, a].rearrange("p j (m t) -> p m j t", t=PACK)[:, m0:m1, :, t0:t1],
             )
 
         def quantise_w1(rounded, b, a, t0, t1):
             cols = slice(t0 * P, t1 * P)
             nc.vector.quantize_mx(out=w1_codes[b, a][:, cols].bitcast(E4M3), scales=w1_scales[b, a][:, cols], in_=rounded[:])
 
-        rounded00 = sb("rounded00", [P, PACK * PASS], BF16, tag="rounded", bufs=2)
+        rounded00 = sb("rounded00", [P, PACK * PASS], BF16)
         round_w1(nc.scalar.copy, rounded00, 0, 0, 0, PACK, 0, P)
         quantise_w1(rounded00, 0, 0, 0, PACK)
+        w4_raw_scales = sb("w4_raw_scales", [P, 2, N], U8, tag="rounded00")
+        nc.gpsimd.memset(w4_raw_scales[:].bitcast(I32), 0)
+        for q in range(4):
+            nc.sync.dma_start(
+                w4_raw_scales[32 * q : 32 * q + 4, :, :].bitcast(I32),
+                w4_scales[:, 4 * q : 4 * q + 4, :].rearrange("a r c -> r a c").bitcast(I32),
+            )
 
         v_words1 = []
 
@@ -143,7 +148,7 @@ def tile_list_baptism_linking_features_kernel(
         def first_stage(i):
             b, t = divmod(i, PACK)
             cols = slice(t * P, (t + 1) * P)
-            th[i] = sb(f"th{i}", [P, S], F32, tag="wide", bufs=6)
+            th[i] = sb(f"th{i}", [P, S], F32, tag="wide", bufs=5)
             for c in range(S // BANK):
                 span = slice(c * BANK, (c + 1) * BANK)
                 acc = psum.tile([P, BANK], F32, name=f"pre{i}_{c}", tag="bank")

@@ -19,11 +19,17 @@ ALU = mybir.AluOpType
 P = 128
 PACK = 4
 PASS = P * PACK
+PASSES = 2
+QUADRANT = 32
+ROWS = 4
 BANK = 512
 LIST = 16
 TILES = H // P
-HALF = 256
+AHEAD = 2
+WIDE_BUFS = 6
+A1_BUFS = 5
 CHUNKS = ((0, 256), (256, 384), (384, 512))
+WIDEST = 256
 
 
 def tile_list_baptism_linking_features_kernel(
@@ -32,7 +38,7 @@ def tile_list_baptism_linking_features_kernel(
     nc = tc.nc
     with ExitStack() as ctx:
         pool = ctx.enter_context(tc.tile_pool(name="sbuf", bufs=1))
-        psum = ctx.enter_context(tc.psum_pool(name="psum", bufs=8))
+        psum = ctx.enter_context(tc.psum_pool(name="psum", bufs=4))
 
         def sb(name, shape, dtype, tag=None, bufs=1):
             return pool.tile(shape, dtype, name=name, tag=tag or name, bufs=bufs, align_bytes=64)
@@ -40,9 +46,12 @@ def tile_list_baptism_linking_features_kernel(
         def entries(offsets, first, last):
             return offsets[:, first // LIST : last // LIST]
 
+        def plane_rows(quadrant):
+            return slice(QUADRANT * quadrant, QUADRANT * quadrant + ROWS)
+
         idx = sb("idx", [P, S // LIST], U16)
         nc.sync.dma_start(idx[:], offs)
-        scale_rows = sb("scale_rows", [P, T], U8, tag="scale_rows")
+        scale_rows = sb("scale_rows", [P, T], U8)
         nc.sync.dma_start(scale_rows[0:32, :].bitcast(I32), tab_scales.rearrange("a q t -> (a q) t").bitcast(I32))
         nc.vector.memset(scale_rows[32:64, :].bitcast(I32), 0)
         nc.vector.memset(scale_rows[64:128, :].bitcast(I32), 0)
@@ -57,75 +66,64 @@ def tile_list_baptism_linking_features_kernel(
 
         gain_t = sb("gain_t", [P, TILES], F32)
         bias_t = sb("bias_t", [P, TILES], F32)
-        nc.gpsimd.dma_start(gain_t[:].rearrange("p (b t) -> p b t", t=PACK), gain.rearrange("(b p t) -> p b t", p=P, t=PACK))
-        nc.gpsimd.dma_start(bias_t[:].rearrange("p (b t) -> p b t", t=PACK), b1.rearrange("(b p t) -> p b t", p=P, t=PACK))
+        for by_tile, vector in ((gain_t, gain), (bias_t, b1)):
+            nc.gpsimd.dma_start(
+                by_tile[:].rearrange("p (b t) -> p b t", t=PACK), vector.rearrange("(b p t) -> p b t", p=P, t=PACK)
+            )
 
-        table = [sb(f"table{a}", [P, T], I32) for a in range(2)]
-        w1_raw = {}
-
-        def load_table(a):
+        table = [sb(f"table{a}", [P, T], I32) for a in range(PASSES)]
+        for a in range(PASSES):
             nc.sync.dma_start(table[a][:], tab_words[a].rearrange("p t i -> p (t i)").bitcast(I32))
+
+        w1_raw = {}
 
         def load_w1(b, a, raw):
             w1_raw[b, a] = raw
             rows = w1[a * PASS : (a + 1) * PASS, b * PASS : (b + 1) * PASS]
             nc.sync.dma_start(raw, rows.rearrange("(p j) c -> p j c", j=PACK))
 
-        load_table(0)
-        load_w1(0, 0, sb("w1_raw00", [P, PACK, PASS], F32, tag="wide", bufs=5)[:])
-        load_table(1)
+        for a in range(PASSES):
+            load_w1(0, a, sb(f"w1_raw0{a}", [P, PACK, PASS], F32, tag="wide", bufs=WIDE_BUFS)[:])
 
-        v_scales = [sb(f"v_scales{a}", [P, S], U8) for a in range(2)]
-        for a in range(2):
+        v_scales = [sb(f"v_scales{a}", [P, S], U8) for a in range(PASSES)]
+        for a in range(PASSES):
             nc.gpsimd.memset(v_scales[a][:].bitcast(I32), 0)
 
-        gain_wide = sb("gain_wide", [P, TILES, HALF], F32)
-        nc.scalar.copy(gain_wide[:], gain_t[:].unsqueeze(2).to_broadcast([P, TILES, HALF]))
+        gain_wide = {}
+        for b, width in enumerate((KEPT, WIDEST)):
+            repeated = sb(f"gain_wide{b}", [P, PACK, width], F32)
+            nc.scalar.copy(repeated[:], gain_t[:, PACK * b : PACK * (b + 1)].unsqueeze(2).to_broadcast([P, PACK, width]))
+            for t in range(PACK):
+                gain_wide[PACK * b + t] = repeated[:, t, :]
 
         picked_rows = sb("picked_rows", [P, S], U8)
         nc.vector.tensor_copy(picked_rows[:], scale_rows[:].indirect(idx[:]))
-
-        def move_scale_rows(a, queue):
-            for q in range(4):
-                queue.dma_start(
-                    v_scales[a][32 * q : 32 * q + 4, :].bitcast(I32),
-                    picked_rows[16 * a + 4 * q : 16 * a + 4 * q + 4, :].bitcast(I32),
-                )
-
-        move_scale_rows(0, nc.scalar)
-        load_w1(0, 1, sb("w1_raw01", [P, PACK, PASS], F32, tag="scale_rows")[:])
-        move_scale_rows(1, nc.sync)
+        for a in range(PASSES):
+            for q in range(P // QUADRANT):
+                queue = nc.gpsimd if a == 1 and q >= 2 else nc.scalar
+                row = 16 * a + ROWS * q
+                queue.dma_start(v_scales[a][plane_rows(q), :].bitcast(I32), picked_rows[row : row + ROWS, :].bitcast(I32))
         v_words0 = sb("v_words0", [P, S], U32)
         nc.vector.tensor_copy(v_words0[:], table[0][:].bitcast(U32).indirect(idx[:]))
-        w1_second = sb("w1_second", [P, 2, PACK, PASS], F32, tag="table0")
-        for a in range(2):
-            load_w1(1, a, w1_second[:, a])
-        w4_raw = sb("w4_raw", [P, 2, 2 * N], U8, tag="picked_rows")
-        nc.sync.dma_start(w4_raw[:].bitcast(I32), w4_words.rearrange("a p c -> p a c").bitcast(I32))
 
-        w1_codes = {(b, a): sb(f"w1_codes{b}{a}", [P, PASS], U32) for b in range(2) for a in range(2)}
-        w1_scales = {(b, a): sb(f"w1_scales{b}{a}", [P, PASS], U8) for b in range(2) for a in range(2)}
+        w1_codes, w1_scales = {}, {}
 
-        def round_w1(copy, rounded, b, a, t0, t1, m0, m1):
-            copy(
-                rounded[:].rearrange("p (t m j) -> p m j t", m=P, j=PACK)[:, m0:m1],
-                w1_raw[b, a].rearrange("p j (m t) -> p m j t", t=PACK)[:, m0:m1, :, t0:t1],
-            )
-
-        def quantise_w1(rounded, b, a, t0, t1):
-            cols = slice(t0 * P, t1 * P)
-            nc.vector.quantize_mx(out=w1_codes[b, a][:, cols].bitcast(E4M3), scales=w1_scales[b, a][:, cols], in_=rounded[:])
-
-        rounded00 = sb("rounded00", [P, PACK * PASS], BF16)
-        round_w1(nc.scalar.copy, rounded00, 0, 0, 0, PACK, 0, P)
-        quantise_w1(rounded00, 0, 0, 0, PACK)
-        w4_raw_scales = sb("w4_raw_scales", [P, 2, N], U8, tag="rounded00")
-        nc.gpsimd.memset(w4_raw_scales[:].bitcast(I32), 0)
-        for q in range(4):
-            nc.sync.dma_start(
-                w4_raw_scales[32 * q : 32 * q + 4, :, :].bitcast(I32),
-                w4_scales[:, 4 * q : 4 * q + 4, :].rearrange("a r c -> r a c").bitcast(I32),
-            )
+        def prepare_w1(copies, b, a, t0, t1, rounded_tag, codes_tag):
+            name = f"w1_{b}{a}{t0}"
+            rounded = sb(f"{name}_rounded", [P, (t1 - t0) * PASS], BF16, tag=rounded_tag)
+            for n, copy in enumerate(copies):
+                share = slice(n * P // len(copies), (n + 1) * P // len(copies))
+                copy(
+                    rounded[:].rearrange("p (t m j) -> p m j t", m=P, j=PACK)[:, share],
+                    w1_raw[b, a].rearrange("p j (m t) -> p m j t", t=PACK)[:, share, :, t0:t1],
+                )
+            codes = sb(f"{name}_codes", [P, (t1 - t0) * P], U32, tag=codes_tag)
+            scales = sb(f"{name}_scales", [P, (t1 - t0) * P], U8)
+            nc.vector.quantize_mx(out=codes[:].bitcast(E4M3), scales=scales[:], in_=rounded[:])
+            for t in range(t0, t1):
+                cols = slice((t - t0) * P, (t - t0 + 1) * P)
+                w1_codes[PACK * b + t, a] = codes[:, cols]
+                w1_scales[PACK * b + t, a] = scales[:, cols]
 
         v_words1 = []
 
@@ -133,96 +131,107 @@ def tile_list_baptism_linking_features_kernel(
             v_words1.append(sb(f"v_words1_{c}", [P, BANK], U32, tag=tag))
             nc.vector.tensor_copy(v_words1[c][:], table[1][:].bitcast(U32).indirect(entries(idx, c * BANK, (c + 1) * BANK)))
 
-        for c in range(3):
+        last_span = S // BANK - 1
+        for c in range(last_span):
             gather_words1(c, None)
-        rounded_first = sb("rounded_first", [P, PASS], BF16, tag="first")
-        round_w1(nc.scalar.copy, rounded_first, 0, 1, 0, 1, 0, P)
-        quantise_w1(rounded_first, 0, 1, 0, 1)
-        gather_words1(3, "first")
-        rounded_rest = sb("rounded_rest", [P, 3 * PASS], BF16, tag="table1")
-        round_w1(nc.vector.tensor_copy, rounded_rest, 0, 1, 1, PACK, 0, P)
-        quantise_w1(rounded_rest, 0, 1, 1, PACK)
+        prepare_w1([nc.scalar.copy], 0, 0, 0, 2, "first0", None)
+        gather_words1(last_span, "first0")
+        prepare_w1([nc.scalar.copy], 0, 0, 2, PACK, None, "table1")
+        prepare_w1([nc.scalar.copy], 0, 1, 0, 2, "first1", None)
+        prepare_w1([nc.vector.tensor_copy], 0, 1, 2, PACK, "first1", None)
 
-        th = {}
+        w4_raw = sb("w4_raw", [P, PASSES, 2 * N], U8, tag="first1")
+        nc.sync.dma_start(w4_raw[:].bitcast(I32), w4_words.rearrange("a p c -> p a c").bitcast(I32))
+        w4_raw_scales = sb("w4_raw_scales", [P, PASSES, N], U8, tag="table0")
+        nc.gpsimd.memset(w4_raw_scales[:].bitcast(I32), 0)
+        for q in range(P // QUADRANT):
+            nc.sync.dma_start(
+                w4_raw_scales[plane_rows(q), :, :].bitcast(I32),
+                w4_scales[:, ROWS * q : ROWS * (q + 1), :].rearrange("a r c -> r a c").bitcast(I32),
+            )
+        w4_codes = sb("w4_codes", [P, PASSES, 2 * N], U8)
+        w4_planes = sb("w4_planes", [P, PASSES, N], U8)
+        nc.vector.tensor_copy(
+            w4_planes[:].rearrange("p a (t m) -> p a t m", t=PACK),
+            w4_raw_scales[:].rearrange("p a (m t) -> p a t m", t=PACK),
+        )
+        w1_second = sb("w1_second", [P, PASSES, PACK, PASS], F32, tag="table0")
+        for a in range(PASSES):
+            load_w1(1, a, w1_second[:, a])
 
-        def first_stage(i):
-            b, t = divmod(i, PACK)
-            cols = slice(t * P, (t + 1) * P)
-            th[i] = sb(f"th{i}", [P, S], F32, tag="wide", bufs=5)
+        def deal_w4_words():
+            nc.scalar.copy(
+                w4_codes[:].bitcast(U16).rearrange("p a (t m) -> p a t m", t=PACK),
+                w4_raw[:].bitcast(U16).rearrange("p a (m t) -> p a t m", t=PACK),
+            )
+
+        def prepare_w1_second_half():
+            for a in range(PASSES):
+                prepare_w1([nc.scalar.copy] * 2, 1, a, 0, PACK, f"second{a}", None)
+
+        tanh, diff, a1, burial = {}, {}, {}, {}
+
+        def first_product(i):
+            tanh[i] = sb(f"tanh{i}", [P, S], F32, tag="wide", bufs=WIDE_BUFS)
             for c in range(S // BANK):
                 span = slice(c * BANK, (c + 1) * BANK)
-                acc = psum.tile([P, BANK], F32, name=f"pre{i}_{c}", tag="bank")
+                acc = psum.tile([P, BANK], F32, name=f"pre{i}_{c}", tag="pre")
                 for a, words in enumerate((v_words0[:, span], v_words1[c][:])):
                     nc.tensor.matmul_mx(
                         out=acc[:],
-                        lhsT=w1_codes[b, a][:, cols].bitcast(E4M3),
-                        lhsT_scale=w1_scales[b, a][:, cols],
+                        lhsT=w1_codes[i, a].bitcast(E4M3),
+                        lhsT_scale=w1_scales[i, a],
                         rhs=words.bitcast(E4M3),
                         rhs_scale=v_scales[a][:, span],
                         start=(a == 0),
-                        stop=(a == 1),
+                        stop=(a == PASSES - 1),
                     )
-                nc.scalar.activation(th[i][:, span], acc[:], ACT.Tanh, bias=bias_t[:, i : i + 1])
-
-        diff, a1, burial = {}, {}, {}
+                nc.scalar.activation(tanh[i][:, span], acc[:], ACT.Tanh, bias=bias_t[:, i : i + 1])
 
         def gather_burial(out, i, j0, j1):
-            nc.vector.tensor_tensor(out, th[i][:].indirect(entries(p4, j0, j1)), gain_wide[:, i, 0 : j1 - j0], ALU.mult)
+            nc.vector.tensor_tensor(out, tanh[i][:].indirect(entries(p4, j0, j1)), gain_wide[i][:, 0 : j1 - j0], ALU.mult)
 
         def gather_pairs(i):
             one = sb(f"one{i}", [P, PAIRS], F32, tag=f"one{i % 2}")
             diff[i] = sb(f"diff{i}", [P, PAIRS], F32, tag="diff", bufs=2)
             if i < PACK:
-                burial[i] = sb(f"burial{i}", [P, KEPT], F32, tag="burial", bufs=2)
-                nc.vector.tensor_copy(one[:], th[i][:].indirect(p1[:]))
-                for j0 in range(0, KEPT, HALF):
-                    gather_burial(burial[i][:, j0 : j0 + HALF], i, j0, j0 + HALF)
-                nc.vector.tensor_tensor(diff[i][:], th[i][:].indirect(p2[:]), one[:], ALU.subtract)
+                burial[i] = sb(f"burial{i}", [P, KEPT], F32, tag=f"burial{i % 2}")
+                nc.vector.tensor_copy(one[:], tanh[i][:].indirect(p1[:]))
+                gather_burial(burial[i][:], i, 0, KEPT)
+                nc.vector.tensor_tensor(diff[i][:], tanh[i][:].indirect(p2[:]), one[:], ALU.subtract)
             else:
                 halves = [(m0, m0 + PAIRS // 2) for m0 in range(0, PAIRS, PAIRS // 2)]
                 for m0, m1 in halves:
-                    nc.vector.tensor_copy(one[:, m0:m1], th[i][:].indirect(entries(p1, m0, m1)))
+                    nc.vector.tensor_copy(one[:, m0:m1], tanh[i][:].indirect(entries(p1, m0, m1)))
                 for m0, m1 in halves:
-                    nc.vector.tensor_tensor(diff[i][:, m0:m1], th[i][:].indirect(entries(p2, m0, m1)), one[:, m0:m1], ALU.subtract)
+                    nc.vector.tensor_tensor(
+                        diff[i][:, m0:m1], tanh[i][:].indirect(entries(p2, m0, m1)), one[:, m0:m1], ALU.subtract
+                    )
 
         def absolute(i):
-            a1[i] = sb(f"a1_{i}", [P, PAIRS], F32, tag="a1", bufs=5)
+            a1[i] = sb(f"a1_{i}", [P, PAIRS], F32, tag="a1", bufs=A1_BUFS)
             nc.scalar.activation(a1[i][:], diff[i][:], ACT.Abs, scale=gain_t[:, i : i + 1])
-
-        def interleave(copy, rounded, planes):
-            copy(rounded.rearrange("p (c i t) -> p c t i", i=4, t=PACK), planes.rearrange("p t (c i) -> p c t i", i=4))
 
         a2_first = sb("a2_first", [P, PACK, KEPT], F32)
 
         def join_first(i):
             nc.vector.tensor_tensor(a2_first[:, i, :], a1[i][:].indirect(p3[:]), burial[i][:], ALU.add)
 
-        def prepare_w1_second():
-            for a in range(2):
-                rounded = sb(f"rounded1{a}", [P, PACK * PASS], BF16, tag="rounded", bufs=2)
-                for m0 in range(0, P, P // 2):
-                    round_w1(nc.scalar.copy, rounded, 1, a, 0, PACK, m0, m0 + P // 2)
-                quantise_w1(rounded, 1, a, 0, PACK)
+        def interleave(copy, rounded, by_tile):
+            copy(rounded.rearrange("p (c i t) -> p c t i", i=4, t=PACK), by_tile.rearrange("p t (c i) -> p c t i", i=4))
 
-        w4_codes = sb("w4_codes", [P, 2, 2 * N], U8)
-        w4_planes = sb("w4_planes", [P, 2, N], U8)
-
-        def deal_w4():
-            nc.vector.tensor_copy(
-                w4_planes[:].rearrange("p a (t m) -> p a t m", t=PACK),
-                w4_raw_scales[:].rearrange("p a (m t) -> p a t m", t=PACK),
-            )
-            nc.scalar.copy(
-                w4_codes[:].bitcast(U16).rearrange("p a (t m) -> p a t m", t=PACK),
-                w4_raw[:].bitcast(U16).rearrange("p a (m t) -> p a t m", t=PACK),
-            )
+        def quantise_a2(name, rounded, width):
+            codes = sb(f"{name}_codes", [P, width], U32)
+            scales = sb(f"{name}_scales", [P, width], U8)
+            nc.vector.quantize_mx(out=codes[:].bitcast(E4M3), scales=scales[:], in_=rounded[:])
+            return codes, scales
 
         y_banks = {}
 
-        def second_stage(b, codes, scales, j0, j1):
+        def second_product(b, codes, scales, j0, j1):
             for jb in range(j0, j1, P):
                 if b == 0:
-                    y_banks[jb] = psum.tile([P, BANK], F32, name=f"y{jb}", tag="bank")
+                    y_banks[jb] = psum.tile([P, BANK], F32, name=f"y{jb}", tag="y")
                 cols = slice(jb - j0, jb - j0 + P)
                 for t in range(PACK):
                     nc.tensor.matmul_mx(
@@ -232,37 +241,29 @@ def tile_list_baptism_linking_features_kernel(
                         rhs=codes[:, cols].bitcast(E4M3),
                         rhs_scale=scales[:, cols],
                         start=(b == 0 and t == 0),
-                        stop=(b == 1 and t == PACK - 1),
+                        stop=(b == PASSES - 1 and t == PACK - 1),
                     )
 
-        def quantise_a2(name, rounded, width):
-            codes = sb(f"{name}_codes", [P, width], U32)
-            scales = sb(f"{name}_scales", [P, width], U8)
-            nc.vector.quantize_mx(out=codes[:].bitcast(E4M3), scales=scales[:], in_=rounded[:])
-            return codes, scales
-
-        def first_pass_of_second_stage():
-            rounded = sb("a2_first_rounded", [P, PACK * KEPT], BF16, tag="rounded", bufs=2)
-            for j0 in range(0, KEPT, HALF):
-                interleave(nc.scalar.copy, rounded[:, PACK * j0 : PACK * (j0 + HALF)], a2_first[:, :, j0 : j0 + HALF])
+        def second_product_first_pass():
+            rounded = sb("a2_first_rounded", [P, PACK * KEPT], BF16, tag="second0")
+            for j0 in range(0, KEPT, WIDEST):
+                interleave(nc.scalar.copy, rounded[:, PACK * j0 : PACK * (j0 + WIDEST)], a2_first[:, :, j0 : j0 + WIDEST])
             codes, scales = quantise_a2("a2_first", rounded, KEPT)
-            second_stage(0, codes, scales, 0, KEPT)
+            second_product(0, codes, scales, 0, KEPT)
 
-        first_stage(0)
-        first_stage(1)
+        side_work = {0: prepare_w1_second_half, 1: deal_w4_words, TILES - AHEAD - 1: second_product_first_pass}
+
+        for i in range(AHEAD):
+            first_product(i)
         for i in range(TILES):
             gather_pairs(i)
             if 1 <= i <= PACK:
                 join_first(i - 1)
-            if i + 2 < TILES:
-                first_stage(i + 2)
+            if i + AHEAD < TILES:
+                first_product(i + AHEAD)
             absolute(i)
-            if i == 0:
-                prepare_w1_second()
-            if i == 1:
-                deal_w4()
-            if i == 5:
-                first_pass_of_second_stage()
+            if i in side_work:
+                side_work[i]()
 
         y_codes = sb("y_codes", [P, KEPT], U32)
         y_scales = sb("y_scales", [P, KEPT], U8)
@@ -280,7 +281,9 @@ def tile_list_baptism_linking_features_kernel(
             j0, j1 = CHUNKS[c]
             joined[c] = sb(f"joined{c}", [P, PACK, j1 - j0], F32, tag=f"chain{c}")
             for t in range(PACK):
-                nc.vector.tensor_tensor(joined[c][:, t, :], a1[PACK + t][:].indirect(entries(p3, j0, j1)), held[c][:, t, :], ALU.add)
+                nc.vector.tensor_tensor(
+                    joined[c][:, t, :], a1[PACK + t][:].indirect(entries(p3, j0, j1)), held[c][:, t, :], ALU.add
+                )
 
         def round_chunk(c, copy):
             j0, j1 = CHUNKS[c]
@@ -290,7 +293,7 @@ def tile_list_baptism_linking_features_kernel(
         def multiply_chunk(c):
             j0, j1 = CHUNKS[c]
             codes, scales = quantise_a2(f"a2_{c}", rounded_a2[c], j1 - j0)
-            second_stage(1, codes, scales, j0, j1)
+            second_product(1, codes, scales, j0, j1)
 
         def round_y(c, copy):
             j0, j1 = CHUNKS[c]
@@ -322,17 +325,18 @@ def tile_list_baptism_linking_features_kernel(
         round_chunk(1, nc.scalar.copy)
         round_y(0, nc.scalar.copy)
         burial_chunk(2)
-        quantise_y(0)
         multiply_chunk(1)
         join_chunk(2)
         round_y(1, nc.scalar.copy)
         store_y(0, nc.sync)
         round_chunk(2, nc.vector.tensor_copy)
-        quantise_y(1)
+        quantise_y(0)
         multiply_chunk(2)
+        quantise_y(1)
         store_y(1, nc.sync)
         round_y(2, nc.vector.tensor_copy)
         store_y(2, nc.scalar)
         quantise_y(2)
-        for q in range(4):
-            nc.sync.dma_start(out_2[0, 4 * q : 4 * q + 4, :].bitcast(I32), y_scales[32 * q : 32 * q + 4, :].bitcast(I32))
+        for q in range(P // QUADRANT):
+            queue = (nc.sync, nc.scalar)[q % 2]
+            queue.dma_start(out_2[0, ROWS * q : ROWS * (q + 1), :].bitcast(I32), y_scales[plane_rows(q), :].bitcast(I32))

from contextlib import ExitStack

import concourse.mybir as mybir

T, S, PAIRS, KEPT, K, H, N = 4096, 2048, 1024, 512, 1024, 1024, 512
FLOPS = 2 * K * H * S + 2 * H * N * KEPT

F32 = mybir.dt.float32
BF16 = mybir.dt.bfloat16
I32 = mybir.dt.int32
U32 = mybir.dt.uint32
U16 = mybir.dt.uint16
U8 = mybir.dt.uint8
E4M3 = mybir.dt.float8_e4m3fn_x4
E2M1 = mybir.dt.float4_e2m1fn_x4
ACT = mybir.ActivationFunctionType
ALU = mybir.AluOpType

P = 128
PACK = 4
PASS = P * PACK
PASSES = 2
QUADRANT = 32
ROWS = 4
BANK = 512
LIST = 16
TILES = H // P
AHEAD = 2
WIDE_BUFS = 6
A1_BUFS = 5
CHUNKS = ((0, 256), (256, 384), (384, 512))
WIDEST = 256


def tile_list_baptism_linking_features_kernel(
    tc, tab_words, tab_scales, offs, pos1, pos2, pos3, pos4, w1, b1, gain, w4_words, w4_scales, out_0, out_1, out_2
):
    nc = tc.nc
    with ExitStack() as ctx:
        pool = ctx.enter_context(tc.tile_pool(name="sbuf", bufs=1))
        psum = ctx.enter_context(tc.psum_pool(name="psum", bufs=4))

        def sb(name, shape, dtype, tag=None, bufs=1):
            return pool.tile(shape, dtype, name=name, tag=tag or name, bufs=bufs, align_bytes=64)

        def entries(offsets, first, last):
            return offsets[:, first // LIST : last // LIST]

        def plane_rows(quadrant):
            return slice(QUADRANT * quadrant, QUADRANT * quadrant + ROWS)

        idx = sb("idx", [P, S // LIST], U16)
        nc.sync.dma_start(idx[:], offs)
        scale_rows = sb("scale_rows", [P, T], U8)
        nc.sync.dma_start(scale_rows[0:32, :].bitcast(I32), tab_scales.rearrange("a q t -> (a q) t").bitcast(I32))
        nc.vector.memset(scale_rows[32:64, :].bitcast(I32), 0)
        nc.vector.memset(scale_rows[64:128, :].bitcast(I32), 0)
        p1 = sb("p1", [P, PAIRS // LIST], U16)
        p2 = sb("p2", [P, PAIRS // LIST], U16)
        p3 = sb("p3", [P, KEPT // LIST], U16)
        p4 = sb("p4", [P, KEPT // LIST], U16)
        nc.sync.dma_start(p1[:], pos1)
        nc.sync.dma_start(p2[:], pos2)
        nc.sync.dma_start(p4[:], pos4)
        nc.sync.dma_start(p3[:], pos3)

        gain_t = sb("gain_t", [P, TILES], F32)
        bias_t = sb("bias_t", [P, TILES], F32)
        for by_tile, vector in ((gain_t, gain), (bias_t, b1)):
            nc.gpsimd.dma_start(
                by_tile[:].rearrange("p (b t) -> p b t", t=PACK), vector.rearrange("(b p t) -> p b t", p=P, t=PACK)
            )

        table = [sb(f"table{a}", [P, T], I32) for a in range(PASSES)]
        for a in range(PASSES):
            nc.sync.dma_start(table[a][:], tab_words[a].rearrange("p t i -> p (t i)").bitcast(I32))

        w1_raw = {}

        def load_w1(b, a, raw):
            w1_raw[b, a] = raw
            rows = w1[a * PASS : (a + 1) * PASS, b * PASS : (b + 1) * PASS]
            nc.sync.dma_start(raw, rows.rearrange("(p j) c -> p j c", j=PACK))

        for a in range(PASSES):
            load_w1(0, a, sb(f"w1_raw0{a}", [P, PACK, PASS], F32, tag="wide", bufs=WIDE_BUFS)[:])

        v_scales = [sb(f"v_scales{a}", [P, S], U8) for a in range(PASSES)]
        for a in range(PASSES):
            nc.gpsimd.memset(v_scales[a][:].bitcast(I32), 0)

        gain_wide = {}
        for b, width in enumerate((KEPT, WIDEST)):
            repeated = sb(f"gain_wide{b}", [P, PACK, width], F32)
            nc.scalar.copy(repeated[:], gain_t[:, PACK * b : PACK * (b + 1)].unsqueeze(2).to_broadcast([P, PACK, width]))
            for t in range(PACK):
                gain_wide[PACK * b + t] = repeated[:, t, :]

        picked_rows = sb("picked_rows", [P, S], U8)
        nc.vector.tensor_copy(picked_rows[:], scale_rows[:].indirect(idx[:]))
        for a in range(PASSES):
            for q in range(P // QUADRANT):
                queue = nc.gpsimd if a == 1 and q >= 2 else nc.scalar
                row = 16 * a + ROWS * q
                queue.dma_start(v_scales[a][plane_rows(q), :].bitcast(I32), picked_rows[row : row + ROWS, :].bitcast(I32))
        v_words0 = sb("v_words0", [P, S], U32)
        nc.vector.tensor_copy(v_words0[:], table[0][:].bitcast(U32).indirect(idx[:]))

        w1_codes, w1_scales = {}, {}

        def prepare_w1(copies, b, a, t0, t1, rounded_tag, codes_tag):
            name = f"w1_{b}{a}{t0}"
            rounded = sb(f"{name}_rounded", [P, (t1 - t0) * PASS], BF16, tag=rounded_tag)
            for n, copy in enumerate(copies):
                share = slice(n * P // len(copies), (n + 1) * P // len(copies))
                copy(
                    rounded[:].rearrange("p (t m j) -> p m j t", m=P, j=PACK)[:, share],
                    w1_raw[b, a].rearrange("p j (m t) -> p m j t", t=PACK)[:, share, :, t0:t1],
                )
            codes = sb(f"{name}_codes", [P, (t1 - t0) * P], U32, tag=codes_tag)
            scales = sb(f"{name}_scales", [P, (t1 - t0) * P], U8)
            nc.vector.quantize_mx(out=codes[:].bitcast(E4M3), scales=scales[:], in_=rounded[:])
            for t in range(t0, t1):
                cols = slice((t - t0) * P, (t - t0 + 1) * P)
                w1_codes[PACK * b + t, a] = codes[:, cols]
                w1_scales[PACK * b + t, a] = scales[:, cols]

        v_words1 = []

        def gather_words1(c, tag):
            v_words1.append(sb(f"v_words1_{c}", [P, BANK], U32, tag=tag))
            nc.vector.tensor_copy(v_words1[c][:], table[1][:].bitcast(U32).indirect(entries(idx, c * BANK, (c + 1) * BANK)))

        last_span = S // BANK - 1
        for c in range(last_span):
            gather_words1(c, None)
        prepare_w1([nc.scalar.copy], 0, 0, 0, 2, "first0", None)
        gather_words1(last_span, "first0")
        prepare_w1([nc.scalar.copy], 0, 0, 2, PACK, None, "table1")
        prepare_w1([nc.scalar.copy], 0, 1, 0, 2, "first1", None)
        prepare_w1([nc.vector.tensor_copy], 0, 1, 2, PACK, "first1", None)

        w4_raw = sb("w4_raw", [P, PASSES, 2 * N], U8, tag="first1")
        nc.sync.dma_start(w4_raw[:].bitcast(I32), w4_words.rearrange("a p c -> p a c").bitcast(I32))
        w4_raw_scales = sb("w4_raw_scales", [P, PASSES, N], U8, tag="table0")
        nc.gpsimd.memset(w4_raw_scales[:].bitcast(I32), 0)
        for q in range(P // QUADRANT):
            nc.sync.dma_start(
                w4_raw_scales[plane_rows(q), :, :].bitcast(I32),
                w4_scales[:, ROWS * q : ROWS * (q + 1), :].rearrange("a r c -> r a c").bitcast(I32),
            )
        w4_codes = sb("w4_codes", [P, PASSES, 2 * N], U8)
        w4_planes = sb("w4_planes", [P, PASSES, N], U8)
        nc.vector.tensor_copy(
            w4_planes[:].rearrange("p a (t m) -> p a t m", t=PACK),
            w4_raw_scales[:].rearrange("p a (m t) -> p a t m", t=PACK),
        )
        w1_second = sb("w1_second", [P, PASSES, PACK, PASS], F32, tag="table0")
        for a in range(PASSES):
            load_w1(1, a, w1_second[:, a])

        def deal_w4_words():
            nc.scalar.copy(
                w4_codes[:].bitcast(U16).rearrange("p a (t m) -> p a t m", t=PACK),
                w4_raw[:].bitcast(U16).rearrange("p a (m t) -> p a t m", t=PACK),
            )

        def prepare_w1_second_half():
            for a in range(PASSES):
                prepare_w1([nc.scalar.copy] * 2, 1, a, 0, PACK, f"second{a}", None)

        tanh, diff, a1, burial = {}, {}, {}, {}

        def first_product(i):
            tanh[i] = sb(f"tanh{i}", [P, S], F32, tag="wide", bufs=WIDE_BUFS)
            for c in range(S // BANK):
                span = slice(c * BANK, (c + 1) * BANK)
                acc = psum.tile([P, BANK], F32, name=f"pre{i}_{c}", tag="pre")
                for a, words in enumerate((v_words0[:, span], v_words1[c][:])):
                    nc.tensor.matmul_mx(
                        out=acc[:],
                        lhsT=w1_codes[i, a].bitcast(E4M3),
                        lhsT_scale=w1_scales[i, a],
                        rhs=words.bitcast(E4M3),
                        rhs_scale=v_scales[a][:, span],
                        start=(a == 0),
                        stop=(a == PASSES - 1),
                    )
                nc.scalar.activation(tanh[i][:, span], acc[:], ACT.Tanh, bias=bias_t[:, i : i + 1])

        def gather_burial(out, i, j0, j1):
            nc.vector.tensor_tensor(out, tanh[i][:].indirect(entries(p4, j0, j1)), gain_wide[i][:, 0 : j1 - j0], ALU.mult)

        def gather_pairs(i):
            one = sb(f"one{i}", [P, PAIRS], F32, tag=f"one{i % 2}")
            diff[i] = sb(f"diff{i}", [P, PAIRS], F32, tag="diff", bufs=2)
            if i < PACK:
                burial[i] = sb(f"burial{i}", [P, KEPT], F32, tag=f"burial{i % 2}")
                nc.vector.tensor_copy(one[:], tanh[i][:].indirect(p1[:]))
                gather_burial(burial[i][:], i, 0, KEPT)
                nc.vector.tensor_tensor(diff[i][:], tanh[i][:].indirect(p2[:]), one[:], ALU.subtract)
            else:
                halves = [(m0, m0 + PAIRS // 2) for m0 in range(0, PAIRS, PAIRS // 2)]
                for m0, m1 in halves:
                    nc.vector.tensor_copy(one[:, m0:m1], tanh[i][:].indirect(entries(p1, m0, m1)))
                for m0, m1 in halves:
                    nc.vector.tensor_tensor(
                        diff[i][:, m0:m1], tanh[i][:].indirect(entries(p2, m0, m1)), one[:, m0:m1], ALU.subtract
                    )

        def absolute(i):
            a1[i] = sb(f"a1_{i}", [P, PAIRS], F32, tag="a1", bufs=A1_BUFS)
            nc.scalar.activation(a1[i][:], diff[i][:], ACT.Abs, scale=gain_t[:, i : i + 1])

        a2_first = sb("a2_first", [P, PACK, KEPT], F32)

        def join_first(i):
            nc.vector.tensor_tensor(a2_first[:, i, :], a1[i][:].indirect(p3[:]), burial[i][:], ALU.add)

        def interleave(copy, rounded, by_tile):
            copy(rounded.rearrange("p (c i t) -> p c t i", i=4, t=PACK), by_tile.rearrange("p t (c i) -> p c t i", i=4))

        def quantise_a2(name, rounded, width):
            codes = sb(f"{name}_codes", [P, width], U32)
            scales = sb(f"{name}_scales", [P, width], U8)
            nc.vector.quantize_mx(out=codes[:].bitcast(E4M3), scales=scales[:], in_=rounded[:])
            return codes, scales

        y_banks = {}

        def second_product(b, codes, scales, j0, j1):
            for jb in range(j0, j1, P):
                if b == 0:
                    y_banks[jb] = psum.tile([P, BANK], F32, name=f"y{jb}", tag="y")
                cols = slice(jb - j0, jb - j0 + P)
                for t in range(PACK):
                    nc.tensor.matmul_mx(
                        out=y_banks[jb][:, t * P : (t + 1) * P],
                        lhsT=w4_codes[:, b, 2 * t * P : 2 * (t + 1) * P].bitcast(E2M1),
                        lhsT_scale=w4_planes[:, b, t * P : (t + 1) * P],
                        rhs=codes[:, cols].bitcast(E4M3),
                        rhs_scale=scales[:, cols],
                        start=(b == 0 and t == 0),
                        stop=(b == PASSES - 1 and t == PACK - 1),
                    )

        def second_product_first_pass():
            rounded = sb("a2_first_rounded", [P, PACK * KEPT], BF16, tag="second0")
            for j0 in range(0, KEPT, WIDEST):
                interleave(nc.scalar.copy, rounded[:, PACK * j0 : PACK * (j0 + WIDEST)], a2_first[:, :, j0 : j0 + WIDEST])
            codes, scales = quantise_a2("a2_first", rounded, KEPT)
            second_product(0, codes, scales, 0, KEPT)

        side_work = {0: prepare_w1_second_half, 1: deal_w4_words, TILES - AHEAD - 1: second_product_first_pass}

        for i in range(AHEAD):
            first_product(i)
        for i in range(TILES):
            gather_pairs(i)
            if 1 <= i <= PACK:
                join_first(i - 1)
            if i + AHEAD < TILES:
                first_product(i + AHEAD)
            absolute(i)
            if i in side_work:
                side_work[i]()

        y_codes = sb("y_codes", [P, KEPT], U32)
        y_scales = sb("y_scales", [P, KEPT], U8)
        out_rows = out_0.rearrange("(p t) j -> p t j", t=PACK)
        out_words = out_1[0].rearrange("p m t -> p (m t)").bitcast(I32)
        held, joined, rounded_a2, rounded_y = {}, {}, {}, {}

        def burial_chunk(c):
            j0, j1 = CHUNKS[c]
            held[c] = sb(f"held{c}", [P, PACK, j1 - j0], F32, tag="one1")
            for t in range(PACK):
                gather_burial(held[c][:, t, :], PACK + t, j0, j1)

        def join_chunk(c):
            j0, j1 = CHUNKS[c]
            joined[c] = sb(f"joined{c}", [P, PACK, j1 - j0], F32, tag=f"chain{c}")
            for t in range(PACK):
                nc.vector.tensor_tensor(
                    joined[c][:, t, :], a1[PACK + t][:].indirect(entries(p3, j0, j1)), held[c][:, t, :], ALU.add
                )

        def round_chunk(c, copy):
            j0, j1 = CHUNKS[c]
            rounded_a2[c] = sb(f"rounded_a2_{c}", [P, PACK * (j1 - j0)], BF16, tag=f"chain{c + 1}")
            interleave(copy, rounded_a2[c][:], joined[c][:])

        def multiply_chunk(c):
            j0, j1 = CHUNKS[c]
            codes, scales = quantise_a2(f"a2_{c}", rounded_a2[c], j1 - j0)
            second_product(1, codes, scales, j0, j1)

        def round_y(c, copy):
            j0, j1 = CHUNKS[c]
            rounded_y[c] = sb(f"rounded_y{c}", [P, PACK * (j1 - j0)], BF16)
            for jb in range(j0, j1, P):
                copy(
                    rounded_y[c][:, PACK * (jb - j0) : PACK * (jb - j0 + P)].rearrange("p (j t) -> p j t", t=PACK),
                    y_banks[jb][:].rearrange("p (t j) -> p j t", t=PACK),
                )

        def quantise_y(c):
            j0, j1 = CHUNKS[c]
            nc.vector.quantize_mx(out=y_codes[:, j0:j1].bitcast(E4M3), scales=y_scales[:, j0:j1], in_=rounded_y[c][:])
            nc.sync.dma_start(out_words[:, j0:j1], y_codes[:, j0:j1].bitcast(I32))

        def store_y(c, queue):
            j0, j1 = CHUNKS[c]
            y = sb(f"y_out{c}", [P, PACK, j1 - j0], F32)
            for jb in range(j0, j1, P):
                nc.scalar.copy(y[:, :, jb - j0 : jb - j0 + P], y_banks[jb][:].rearrange("p (t j) -> p t j", t=PACK))
            queue.dma_start(out_rows[:, :, j0:j1], y[:])

        burial_chunk(0)
        join_chunk(0)
        round_chunk(0, nc.scalar.copy)
        burial_chunk(1)
        multiply_chunk(0)
        join_chunk(1)
        round_chunk(1, nc.scalar.copy)
        round_y(0, nc.scalar.copy)
        burial_chunk(2)
        multiply_chunk(1)
        join_chunk(2)
        round_y(1, nc.scalar.copy)
        store_y(0, nc.sync)
        round_chunk(2, nc.vector.tensor_copy)
        quantise_y(0)
        multiply_chunk(2)
        quantise_y(1)
        store_y(1, nc.sync)
        round_y(2, nc.vector.tensor_copy)
        store_y(2, nc.scalar)
        quantise_y(2)
        for q in range(P // QUADRANT):
            queue = (nc.sync, nc.scalar)[q % 2]
            queue.dma_start(out_2[0, ROWS * q : ROWS * (q + 1), :].bitcast(I32), y_scales[plane_rows(q), :].bitcast(I32))
